import numpy as np, ml_dtypes
CORES = [113,118,241,246]
N = 4
GR, GC, HH, WW = 2, 2, 4, 64
def setup_inputs(rng):
    return {"x": rng.standard_normal((N, 128, HH * WW), dtype=np.float32).astype(ml_dtypes.bfloat16), "w": rng.standard_normal((N, 128, 9 * 128), dtype=np.float32).astype(ml_dtypes.bfloat16)}
def setup_inputs_big(rng):
    d = setup_inputs(rng)
    for k in ("x", "w"): d[k] = (d[k].astype(np.float32) * 1024.0).astype(d[k].dtype)
    return d
def setup_inputs_small(rng):
    d = setup_inputs(rng)
    for k in ("x", "w"): d[k] = (d[k].astype(np.float32) * (1 / 1024.0)).astype(d[k].dtype)
    return d
def setup_inputs_apart(rng):
    d = setup_inputs(rng)
    f = (10.0 ** rng.permutation(np.linspace(-1.5, 1.5, N))).astype(np.float32).reshape(N, 1, 1)
    for k in ("x", "w"): d[k] = (d[k].astype(np.float32) * f).astype(d[k].dtype)
    return d
def reference(x, w):
    X = x.astype(np.float64).reshape(GR, GC, 128, HH, WW); W = w.astype(np.float64)
    g = np.concatenate([np.concatenate(list(X[i]), axis=2) for i in range(GR)], axis=1)
    y = np.zeros((N, 128, HH * WW))
    for r in range(N):
        i0, j0 = HH * (r // GC), WW * (r % GC)
        for a in range(3):
            for b in range(3):
                sh = np.roll(g, (-2 * (a - 1), -2 * (b - 1)), axis=(1, 2))[:, i0:i0 + HH, j0:j0 + WW]
                y[r] += W[r][:, 128 * (3 * a + b):128 * (3 * a + b) + 128].T @ sh.reshape(128, HH * WW)
    return {"y": y.astype(ml_dtypes.bfloat16 if x.dtype != np.float64 else np.float64)}

from concourse.bass import DstId, RemoteDMATransfer

GR, GC, HH, WW = 2, 2, 4, 64
P = 128
E = 2

SCRATCH = {
    "xs": ("sbuf", [P, HH, WW], "bfloat16"),
    "vt": ("sbuf", [P, HH, WW], "bfloat16"),
    "hp": ("sbuf", [P, HH, 2 * E], "bfloat16"),
    "hal": ("sbuf", [P, 2 * HH, 2 * E], "bfloat16"),
    "ws": ("sbuf", [P, 9 * P], "bfloat16"),
    "ob": ("sbuf", [P, HH, WW], "bfloat16"),
    "ps": ("psum", [P, HH, WW], "float32"),
}
SEMAPHORES = ["sx", "sw", "sp", "sl", "sv", "sh", "sd", "sm", "so", "sy"]


def _count(mask):
    n = 0
    while mask:
        n += mask & 1
        mask >>= 1
    return n


def rank_program(g, core, T, topo):
    r = T.rank_of(core)
    if r is None:
        return
    S = T.sem
    gr, gc = r // GC, r % GC
    V = T.cores[((gr + 1) % GR) * GC + gc]
    H = T.cores[gr * GC + (gc + 1) % GC]
    D = T.cores[((gr + 1) % GR) * GC + (gc + 1) % GC]

    m_v = topo.mask(core, V)
    m_d = topo.mask(core, D)
    m_h = topo.mask(core, H) & ~(m_v | m_d)
    n_v, n_d, n_h = _count(m_v), _count(m_d), _count(m_h)

    g.sync.dma_start(T.xs[:, :, :], T.x[:, :]).then_inc(S.sx, 16)
    g.sync.dma_start(T.ws[:, :], T.w[:, :]).then_inc(S.sw, 16)

    g.vector.wait_ge(S.sx, 16)
    g.vector.tensor_copy(T.hp[:, :, 0:E], T.xs[:, :, WW - E:WW]).then_inc(S.sp, 1)
    g.vector.tensor_copy(T.hp[:, :, E:2 * E], T.xs[:, :, 0:E]).then_inc(S.sp, 1)

    g.wait_ge(S.sx, 16)
    rid, pid = topo.addr(V, core)
    g.remote_dma(T.vt[:, :, :], T.xs[:, :, :], remote_sem=S.sv, local_sem=S.sl, pid=pid, routing_id=rid,
                 dma_engine_mask=m_v)
    g.wait_ge(S.sp, 2)
    rid_d, pid_d = topo.addr(D, core)
    rid_h, pid_h = topo.addr(H, core)
    g.remote_dma_fused([
        RemoteDMATransfer(dst_ids=[DstId(rid=rid_d, pnc=pid_d)], dma_engine_mask=m_d, remote_sem=S.sd,
                          src=T.hp[:, :, :], dst=T.hal[:, HH:2 * HH, :]),
        RemoteDMATransfer(dst_ids=[DstId(rid=rid_h, pnc=pid_h)], dma_engine_mask=m_h, remote_sem=S.sh,
                          src=T.hp[:, :, :], dst=T.hal[:, 0:HH, :]),
    ], local_sem=S.sl)

    done = [0]

    def mm(a, b, ro, co, src, rs, cs, start=False, stop=False):
        k = 3 * a + b
        g.tensor.matmul(T.ps[:, ro[0]:ro[1], co[0]:co[1]], T.ws[:, P * k:P * (k + 1)],
                        src[:, rs[0]:rs[1], cs[0]:cs[1]], start, stop).then_inc(S.sm, 1)
        done[0] += 1

    inner = {1: ((0, WW), (0, WW)), 0: ((E, WW), (0, WW - E)), 2: ((0, WW - E), (E, WW))}
    edge = {0: ((0, E), (0, E)), 2: ((WW - E, WW), (E, 2 * E))}

    g.tensor.wait_ge(S.sx, 16)
    g.tensor.wait_ge(S.sw, 16)
    first = True
    for a, ro, rs in ((1, (0, HH), (0, HH)), (0, (E, HH), (0, HH - E)), (2, (0, HH - E), (E, HH))):
        for b in (1, 0, 2):
            mm(a, b, ro, inner[b][0], T.xs, rs, inner[b][1], start=first)
            first = False
    g.tensor.wait_ge(S.sv, n_v)
    for a, ro, rs in ((0, (0, E), (HH - E, HH)), (2, (HH - E, HH), (0, E))):
        for b in (1, 0, 2):
            mm(a, b, ro, inner[b][0], T.vt, rs, inner[b][1])
    g.tensor.wait_ge(S.sh, n_h)
    for a, ro, rs in ((1, (0, HH), (0, HH)), (0, (E, HH), (0, HH - E))):
        for b in (0, 2):
            mm(a, b, ro, edge[b][0], T.hal, rs, edge[b][1])
    g.tensor.wait_ge(S.sd, n_d)
    mm(0, 0, (0, E), edge[0][0], T.hal, (2 * HH - E, 2 * HH), edge[0][1])
    mm(0, 2, (0, E), edge[2][0], T.hal, (2 * HH - E, 2 * HH), edge[2][1])
    mm(2, 0, (0, HH), edge[0][0], T.hal, (E, E + HH), edge[0][1])
    mm(2, 2, (0, HH), edge[2][0], T.hal, (E, E + HH), edge[2][1], stop=True)

    g.vector.wait_ge(S.sm, done[0])
    g.vector.tensor_copy(T.ob[:, :, :], T.ps[:, :, :]).then_inc(S.so, 1)
    g.sync.wait_ge(S.so, 1)
    g.sync.dma_start(T.y[:, :], T.ob[:, :, :]).then_inc(S.sy, 16)
    g.sync.wait_ge(S.sy, 16)

    g.wait_ge(S.sl, n_v + n_d + n_h)
